import numpy as np
import ml_dtypes


def mxq(x, axis, fmt="e4m3"):
    dtype, down = {"e4m3": (ml_dtypes.float8_e4m3fn, 7), "e5m2": (ml_dtypes.float8_e5m2, 14)}[fmt]
    v = np.moveaxis(np.asarray(x, np.float32).astype(ml_dtypes.bfloat16).astype(np.float64), axis, -1)
    blocks = v.reshape(v.shape[:-1] + (-1, 32))
    amax = np.abs(blocks).max(-1, keepdims=True)
    byte = np.maximum(np.where(amax > 0, np.frexp(amax)[1] - 1 + 127, 0) - down, 1)
    scale = np.exp2(byte - 127.0)
    codes = (blocks / scale).astype(np.float32).astype(dtype).astype(np.float64)
    return np.moveaxis((codes * scale).reshape(v.shape), -1, axis)


WIDE = False


def mx_kscale(k):
    if not WIDE:
        return np.ones(k)
    levels = np.array([10, -10, 5, -5, 0])
    if k % 512:
        return np.exp2(np.random.permutation(np.resize(levels, k // 32))).repeat(32)
    a = np.empty((k // 512, 16))
    for p in range(k // 512):
        a[p, :8] = np.random.permutation(np.resize(levels, 8))
        for g in range(8):
            far = levels[np.abs(levels - a[p, g]) >= 10]
            a[p, g + 8] = far[np.random.randint(len(far))]
    return np.exp2(a.ravel()).repeat(32)


def f64(x):
    return np.asarray(x).astype(np.float64)


def striped(idx):
    return np.tile(np.asarray(idx).reshape(-1, 16).T, (8, 1)).astype(np.uint16)


def unstriped(offs):
    return offs[:16].T.reshape(-1).astype(np.int64)


E2M1 = np.array([0.0, 0.5, 1.0, 1.5, 2.0, 3.0, 4.0, 6.0, -0.0, -0.5, -1.0, -1.5, -2.0, -3.0, -4.0, -6.0])


def pack_weight(w, fmt):
    k, n = w.shape
    w = f64(np.asarray(w, np.float32).astype(ml_dtypes.bfloat16)).reshape(k // 32, 32, n)
    amax = np.abs(w).max(1)
    if fmt == "e4m3":
        byte = np.frexp(amax)[1] - 1 + 127 - 7
    else:
        mant, ex = np.frexp(amax / 6.0)
        byte = np.where(mant > 0.5, ex, ex - 1) + 127
    byte = np.clip(np.where(amax > 0, byte, 1), 1, 254)
    scaled = (w * np.exp2(127.0 - byte)[:, None, :]).reshape(k, n).astype(np.float32)
    by_word = np.ascontiguousarray(scaled.reshape(k // 512, 128, 4, n).transpose(0, 1, 3, 2))
    if fmt == "e4m3":
        words = by_word.astype(ml_dtypes.float8_e4m3fn).view(np.uint8)
    else:
        c = by_word.astype(ml_dtypes.float4_e2m1fn).view(np.uint8) & 0xF
        words = (c[..., 0::2] | (c[..., 1::2] << 4)).reshape(k // 512, 128, 2 * n)
    return np.ascontiguousarray(words), np.ascontiguousarray(byte.astype(np.uint8).reshape(k // 512, 16, n))


def unpack_weight(words, scales, fmt):
    g, _, n = scales.shape
    words = np.ascontiguousarray(words).reshape(g, 128, n, -1)
    if fmt == "e4m3":
        vals = words.view(ml_dtypes.float8_e4m3fn).astype(np.float64)
    else:
        nib = np.empty((g, 128, n, 4), np.uint8)
        nib[..., 0::2] = words & 0xF
        nib[..., 1::2] = words >> 4
        vals = E2M1[nib]
    vals = vals * np.repeat(np.exp2(scales.astype(np.float64) - 127.0), 8, axis=1)[..., None]
    return vals.transpose(0, 1, 3, 2).reshape(g * 512, n)


D, T, U, I, J, G = 512, 1024, 1024, 256, 512, 64


def setup_inputs():
    n = np.random.standard_normal
    idx = np.random.permutation(T)[:I]
    idx2 = np.random.permutation(U)[:J]
    fd = mx_kscale(D)
    tabbp = pack_weight(n((D, U)) / fd[:, None], "e4m3")
    return {
        "taba": (n((D, T)) * 1 / np.sqrt(D) * fd[:, None]).astype(np.float32),
        "tabb_words": tabbp[0],
        "tabb_scales": tabbp[1],
        "temper": (np.random.uniform(0.5, 2.0, (I, 1))).astype(np.float32),
        "gw": (n((I, G)) * 1.5).astype(np.float32),
        "old": (0.3 * n((I, J))).astype(np.float32),
        "offs": striped(idx),
        "offs2": striped(idx2),
    }


def reference(taba, tabb_words, tabb_scales, temper, gw, old, offs, offs2):
    idx = unstriped(offs)
    idx2 = unstriped(offs2)
    tabbu = unpack_weight(tabb_words, tabb_scales, "e4m3")
    tabaidxq = mxq(f64(taba)[:, idx], 0, "e4m3")
    tabbidx2g = tabbu[:, idx2]
    s = tabaidxq.T @ tabbidx2g
    p = np.exp(s * f64(temper))
    z = p.reshape(I, G, J // G).sum(axis=2)
    pl1 = np.log(z) / f64(temper)
    dpl1 = f64(gw) * (1.0 - np.square(np.tanh(pl1 - 2.0)))
    dz = dpl1 / f64(temper) / z
    r1 = np.repeat(dz, J // G, axis=1)
    ds = r1 * p * f64(temper)
    y = ds * 4.0 + f64(old)
    return y

@@ -1,0 +1,155 @@
+import math
+from contextlib import ExitStack
+
+import concourse.mybir as mybir
+
+D, T, U, I, J, G = 512, 1024, 1024, 256, 512, 64
+FLOPS = 2 * D * I * J
+
+F32 = mybir.dt.float32
+BF16 = mybir.dt.bfloat16
+I32 = mybir.dt.int32
+U32 = mybir.dt.uint32
+U16 = mybir.dt.uint16
+U8 = mybir.dt.uint8
+FP8X4 = mybir.dt.float8_e4m3fn_x4
+ALU = mybir.AluOpType
+ACT = mybir.ActivationFunctionType
+
+P = 128
+PACK = 4
+HALVES = I // P
+MEMBERS = J // G
+STRIPE = 16
+UNITS = ((0, 256), (256, 512))
+
+LN2_SHORT = round(math.log(2.0) * 2.0**16) / 2.0**16
+BITS_SCALE = LN2_SHORT / 2.0**23
+BITS_ONE = 127.0 * 2.0**23
+CENTRE = 1.08
+
+
+def laguerre(n, t):
+    return sum((-t) ** k * math.factorial(n + 1) / (math.factorial(n - k) * math.factorial(k + 1) * math.factorial(k)) for k in range(n + 1))
+
+
+def laguerre_root(n, low, high):
+    for step in range(60):
+        middle = (low + high) / 2.0
+        low, high = (middle, high) if laguerre(n, low) * laguerre(n, middle) > 0.0 else (low, middle)
+    return low
+
+
+NODES = tuple(laguerre_root(4, low, high) for low, high in ((0.0, 1.0), (1.0, 4.0), (4.0, 8.0), (8.0, 16.0)))
+AMPLITUDES = tuple(1.0 / (5.0 * laguerre(5, t) ** 2 * t) for t in NODES)
+LINEAR = 0.2
+C0 = math.log(CENTRE) - LINEAR + sum(AMPLITUDES)
+TERMS = len(NODES) + 1
+
+
+def tile_attend_blogpool_kernel(tc, taba, tabb_words, tabb_scales, temper, gw, old, offs, offs2, out):
+    nc = tc.nc
+    with ExitStack() as ctx:
+        sb = ctx.enter_context(tc.tile_pool(name="sb", bufs=1))
+        psum = ctx.enter_context(tc.psum_pool(name="psum", bufs=1))
+
+        a_list = sb.tile([P, I // STRIPE], U16, name="a_list")
+        b_list = sb.tile([P, J // STRIPE], U16, name="b_list")
+        b_scales = sb.tile([P, U], U8, name="b_scales", align_bytes=64)
+        b_words = sb.tile([P, U], U32, name="b_words", align_bytes=64)
+        a_rows = [sb.tile([P, T], F32, name="a_rows%d" % t, align_bytes=64) for t in range(PACK)]
+        temper_sb = sb.tile([P, HALVES], F32, name="temper_sb")
+        gw_sb = sb.tile([P, HALVES, G], F32, name="gw_sb")
+        old_sb = sb.tile([P, HALVES, J], F32, name="old_sb")
+
+        nc.vector.memset(b_scales[:].bitcast(I32), 0)
+        ones = sb.tile([P, 1], F32, name="ones")
+        nc.vector.memset(ones[:], 1.0)
+
+        nc.sync.dma_start(b_list[:], offs2)
+        for q in range(4):
+            nc.scalar.dma_start(b_scales[32 * q : 32 * q + 4, :].bitcast(I32), tabb_scales[0, 4 * q : 4 * q + 4, :].bitcast(I32))
+        nc.sync.dma_start(a_list[:], offs)
+        taba_planes = taba.rearrange("(p t) c -> p t c", t=PACK)
+        for t in range(PACK):
+            nc.sync.dma_start(a_rows[t][:], taba_planes[:, t, :])
+        nc.sync.dma_start(b_words[:].bitcast(I32), tabb_words[0].rearrange("p n t -> p (n t)").bitcast(I32))
+        nc.sync.dma_start(temper_sb[:], temper.rearrange("(p h) o -> p (h o)", h=HALVES))
+        nc.sync.dma_start(gw_sb[:], gw.rearrange("(p h) g -> p h g", h=HALVES))
+        nc.sync.dma_start(old_sb[:], old.rearrange("(p h) j -> p h j", h=HALVES))
+
+        biases = sb.tile([P, 6], F32, name="biases")
+        for col, value in enumerate((BITS_ONE * BITS_SCALE, -C0) + tuple(math.log(a) + t for a, t in zip(AMPLITUDES, NODES))):
+            nc.scalar.activation(biases[:, col : col + 1], ones[:], ACT.Copy, scale=value)
+        inv_temper = sb.tile([P, HALVES], F32, name="inv_temper")
+        nc.vector.reciprocal(inv_temper[:], temper_sb[:])
+        tanh_bias = sb.tile([P, HALVES], F32, name="tanh_bias")
+        nc.vector.tensor_scalar(tanh_bias[:], inv_temper[:], -C0, 2.0, ALU.mult, ALU.add)
+
+        bg_scales = sb.tile([P, J], U8, name="bg_scales", align_bytes=64)
+        nc.vector.tensor_copy(bg_scales[:], b_scales[:].indirect(b_list[:]))
+
+        grouped = sb.tile([P, I, PACK], BF16, name="grouped", align_bytes=64)
+        dealt = grouped[:].rearrange("p (h m) t -> p t m h", h=HALVES)
+        for t in range(PACK):
+            nc.vector.tensor_copy(dealt[:, t, :, :], a_rows[t][:].indirect(a_list[:]))
+        a_codes = sb.tile([P, I], U32, name="a_codes", align_bytes=64)
+        a_scales = sb.tile([P, I], U8, name="a_scales", align_bytes=64)
+        nc.vector.quantize_mx(out=a_codes[:].bitcast(FP8X4), scales=a_scales[:], in_=grouped[:].rearrange("p c t -> p (c t)"))
+
+        out_rows = out.rearrange("(p h) j -> p h j", h=HALVES)
+        for u, (j0, j1) in enumerate(UNITS):
+            width = j1 - j0
+            groups = width // MEMBERS
+
+            def small(name):
+                return sb.tile([P, HALVES, groups], F32, name="%s%d" % (name, u))
+
+            bg_words = sb.tile([P, width], U32, name="bg_words%d" % u, align_bytes=64)
+            nc.vector.tensor_copy(bg_words[:], b_words[:].indirect(b_list[:, j0 // STRIPE : j1 // STRIPE]))
+            p = sb.tile([P, HALVES, width], F32, name="p%d" % u)
+            z = small("z")
+            for h in range(HALVES):
+                s = psum.tile([P, width], F32, name="s%d_%d" % (u, h))
+                for c0, c1 in ((0, 256), (256, width)) if width > 256 else ((0, width),):
+                    nc.tensor.matmul_mx(
+                        out=s[:, c0:c1],
+                        lhsT=a_codes[:, h * P : (h + 1) * P].bitcast(FP8X4),
+                        lhsT_scale=a_scales[:, h * P : (h + 1) * P],
+                        rhs=bg_words[:, c0:c1].bitcast(FP8X4),
+                        rhs_scale=bg_scales[:, j0 + c0 : j0 + c1],
+                        start=True,
+                        stop=True,
+                    )
+                nc.scalar.activation(p[:, h, :], s[:], ACT.Exp, scale=temper_sb[:, h : h + 1])
+                nc.vector.tensor_reduce(z[:, h, :], p[:, h, :].rearrange("p (g k) -> p g k", k=MEMBERS), mybir.AxisListType.X, ALU.add)
+
+            inv_guess, guess, w0, y = small("inv_guess"), small("guess"), small("w0"), small("y")
+            terms = sb.tile([P, TERMS, HALVES, groups], F32, name="terms%d" % u)
+            nc.scalar.activation(inv_guess[:], z[:].bitcast(U32), ACT.Exp, bias=biases[:, 0:1], scale=-BITS_SCALE)
+            nc.vector.tensor_scalar(guess[:], z[:].bitcast(I32), -BITS_ONE, BITS_SCALE, ALU.add, ALU.mult)
+            nc.vector.tensor_tensor(w0[:], z[:], inv_guess[:], ALU.mult)
+            for k, t in enumerate(NODES):
+                nc.scalar.activation(terms[:, k], w0[:], ACT.Exp, bias=biases[:, 2 + k : 3 + k], scale=-t / CENTRE)
+            nc.vector.scalar_tensor_tensor(terms[:, TERMS - 1], w0[:], -LINEAR / CENTRE, guess[:], ALU.mult, ALU.subtract)
+            nc.vector.tensor_reduce(y[:].rearrange("p h g -> p (h g)"), terms[:].rearrange("p k h g -> p (h g) k"), mybir.AxisListType.X, ALU.add)
+            th, th2, inv_z, gz, f = small("th"), small("th2"), small("inv_z"), small("gz"), small("f")
+            for h in range(HALVES):
+                nc.scalar.activation(th[:, h, :], y[:, h, :], ACT.Tanh, bias=tanh_bias[:, h : h + 1], scale=inv_temper[:, h : h + 1])
+            nc.scalar.activation(inv_z[:], y[:], ACT.Exp, bias=biases[:, 1:2])
+            nc.scalar.activation(th2[:], th[:], ACT.Square)
+            nc.vector.scalar_tensor_tensor(gz[:], inv_z[:], -4.0, gw_sb[:, :, j0 // MEMBERS : j1 // MEMBERS], ALU.mult, ALU.mult)
+            nc.vector.scalar_tensor_tensor(f[:], th2[:], -1.0, gz[:], ALU.add, ALU.mult)
+
+            ds = [sb.tile([P, groups, MEMBERS], F32, name="ds%d_%d" % (u, h)) for h in range(HALVES)]
+            res = [sb.tile([P, width], F32, name="res%d_%d" % (u, h)) for h in range(HALVES)]
+            for h in range(HALVES):
+                nc.vector.tensor_tensor(
+                    ds[h][:],
+                    p[:, h, :].rearrange("p (g k) -> p g k", k=MEMBERS),
+                    f[:, h, :].unsqueeze(2).to_broadcast([P, groups, MEMBERS]),
+                    ALU.mult,
+                )
+            for h in range(HALVES):
+                nc.vector.tensor_tensor(res[h][:], ds[h][:].rearrange("p g k -> p (g k)"), old_sb[:, h, j0:j1], ALU.add)
+                nc.sync.dma_start(out_rows[:, h, j0:j1], res[h][:])

@@ -21,29 +21,43 @@ PACK = 4
 HALVES = I // P
 MEMBERS = J // G
 STRIPE = 16
-UNITS = ((0, 256), (256, 512))
+UNITS = ((0, 128), (128, 256), (256, 512))
 
 LN2_SHORT = round(math.log(2.0) * 2.0**16) / 2.0**16
 BITS_SCALE = LN2_SHORT / 2.0**23
 BITS_ONE = 127.0 * 2.0**23
-CENTRE = 1.08
+CENTRE = 1.06
+REACH = 0.2
+SPACING = 2.0 * REACH / 7.0
+SAMPLES = tuple(math.log(1.0 - REACH + n * SPACING) for n in range(8))
+CURVES = tuple(2.0 * SAMPLES[n + 1] - SAMPLES[n] - SAMPLES[n + 2] for n in range(6))
 
 
-def laguerre(n, t):
-    return sum((-t) ** k * math.factorial(n + 1) / (math.factorial(n - k) * math.factorial(k + 1) * math.factorial(k)) for k in range(n + 1))
+def det3(m):
+    return sum(m[0][k] * (m[1][(k + 1) % 3] * m[2][(k + 2) % 3] - m[1][(k + 2) % 3] * m[2][(k + 1) % 3]) for k in range(3))
 
 
-def laguerre_root(n, low, high):
+def solve3(m, rhs):
+    return tuple(det3([[rhs[r] if c == k else m[r][c] for c in range(3)] for r in range(3)]) / det3(m) for k in range(3))
+
+
+def bisect_root(poly, low, high):
     for step in range(60):
         middle = (low + high) / 2.0
-        low, high = (middle, high) if laguerre(n, low) * laguerre(n, middle) > 0.0 else (low, middle)
+        low, high = (middle, high) if poly(low) * poly(middle) > 0.0 else (low, middle)
     return low
 
 
-NODES = tuple(laguerre_root(4, low, high) for low, high in ((0.0, 1.0), (1.0, 4.0), (4.0, 8.0), (8.0, 16.0)))
-AMPLITUDES = tuple(1.0 / (5.0 * laguerre(5, t) ** 2 * t) for t in NODES)
-LINEAR = 0.2
-C0 = math.log(CENTRE) - LINEAR + sum(AMPLITUDES)
+RECURRENCE = solve3([CURVES[r : r + 3] for r in range(3)], CURVES[3:6])
+NODES = tuple(
+    bisect_root(lambda t: math.exp(-3.0 * SPACING * t) - sum(c * math.exp(-k * SPACING * t) for k, c in enumerate(RECURRENCE)), low, high)
+    for low, high in ((0.1, 2.0), (2.0, 5.0), (5.0, 12.0))
+)
+CURVE_SHARES = solve3([[math.exp(-r * SPACING * t) for t in NODES] for r in range(3)], CURVES[0:3])
+AMPLITUDES = tuple(a * math.exp(-REACH * t) / (1.0 - math.exp(-SPACING * t)) ** 2 for a, t in zip(CURVE_SHARES, NODES))
+ENDS = tuple(math.log(1.0 + u) + sum(a * math.exp(-t * u) for a, t in zip(AMPLITUDES, NODES)) for u in (-REACH, REACH))
+LINEAR = (ENDS[1] - ENDS[0]) / (2.0 * REACH)
+C0 = math.log(CENTRE) - LINEAR + (ENDS[0] + ENDS[1]) / 2.0
 TERMS = len(NODES) + 1
 
 
@@ -67,6 +81,8 @@ def tile_attend_blogpool_kernel(tc, taba, tabb_words, tabb_scales, temper, gw, o
         nc.vector.memset(ones[:], 1.0)
 
         nc.sync.dma_start(b_list[:], offs2)
+        with nc.allow_non_contiguous_dma(reason="one temper a row"):
+            nc.scalar.dma_start(temper_sb[:], temper.rearrange("(h p) o -> p (h o)", h=HALVES))
         for q in range(4):
             nc.scalar.dma_start(b_scales[32 * q : 32 * q + 4, :].bitcast(I32), tabb_scales[0, 4 * q : 4 * q + 4, :].bitcast(I32))
         nc.sync.dma_start(a_list[:], offs)
@@ -74,12 +90,11 @@ def tile_attend_blogpool_kernel(tc, taba, tabb_words, tabb_scales, temper, gw, o
         for t in range(PACK):
             nc.sync.dma_start(a_rows[t][:], taba_planes[:, t, :])
         nc.sync.dma_start(b_words[:].bitcast(I32), tabb_words[0].rearrange("p n t -> p (n t)").bitcast(I32))
-        nc.sync.dma_start(temper_sb[:], temper.rearrange("(p h) o -> p (h o)", h=HALVES))
-        nc.sync.dma_start(gw_sb[:], gw.rearrange("(p h) g -> p h g", h=HALVES))
-        nc.sync.dma_start(old_sb[:], old.rearrange("(p h) j -> p h j", h=HALVES))
+        nc.sync.dma_start(gw_sb[:], gw.rearrange("(h p) g -> p h g", h=HALVES))
+        nc.sync.dma_start(old_sb[:], old.rearrange("(h p) j -> p h j", h=HALVES))
 
-        biases = sb.tile([P, 6], F32, name="biases")
-        for col, value in enumerate((BITS_ONE * BITS_SCALE, -C0) + tuple(math.log(a) + t for a, t in zip(AMPLITUDES, NODES))):
+        biases = sb.tile([P, 3 + len(NODES)], F32, name="biases")
+        for col, value in enumerate((BITS_ONE * BITS_SCALE, -C0) + tuple(math.log(a) + t for a, t in zip(AMPLITUDES, NODES)) + (-BITS_ONE * BITS_SCALE,)):
             nc.scalar.activation(biases[:, col : col + 1], ones[:], ACT.Copy, scale=value)
         inv_temper = sb.tile([P, HALVES], F32, name="inv_temper")
         nc.vector.reciprocal(inv_temper[:], temper_sb[:])
@@ -90,14 +105,15 @@ def tile_attend_blogpool_kernel(tc, taba, tabb_words, tabb_scales, temper, gw, o
         nc.vector.tensor_copy(bg_scales[:], b_scales[:].indirect(b_list[:]))
 
         grouped = sb.tile([P, I, PACK], BF16, name="grouped", align_bytes=64)
-        dealt = grouped[:].rearrange("p (h m) t -> p t m h", h=HALVES)
+        dealt = grouped[:].rearrange("p c t -> p t c")
         for t in range(PACK):
-            nc.vector.tensor_copy(dealt[:, t, :, :], a_rows[t][:].indirect(a_list[:]))
+            nc.vector.tensor_copy(dealt[:, t, :], a_rows[t][:].indirect(a_list[:]))
         a_codes = sb.tile([P, I], U32, name="a_codes", align_bytes=64)
         a_scales = sb.tile([P, I], U8, name="a_scales", align_bytes=64)
         nc.vector.quantize_mx(out=a_codes[:].bitcast(FP8X4), scales=a_scales[:], in_=grouped[:].rearrange("p c t -> p (c t)"))
 
-        out_rows = out.rearrange("(p h) j -> p h j", h=HALVES)
+        out_rows = out.rearrange("(h p) j -> p h j", h=HALVES)
+        made = []
         for u, (j0, j1) in enumerate(UNITS):
             width = j1 - j0
             groups = width // MEMBERS
@@ -111,7 +127,7 @@ def tile_attend_blogpool_kernel(tc, taba, tabb_words, tabb_scales, temper, gw, o
             z = small("z")
             for h in range(HALVES):
                 s = psum.tile([P, width], F32, name="s%d_%d" % (u, h))
-                for c0, c1 in ((0, 256), (256, width)) if width > 256 else ((0, width),):
+                for c0, c1 in ((0, 128), (128, width)) if width == 192 else ((0, width),):
                     nc.tensor.matmul_mx(
                         out=s[:, c0:c1],
                         lhsT=a_codes[:, h * P : (h + 1) * P].bitcast(FP8X4),
@@ -127,7 +143,7 @@ def tile_attend_blogpool_kernel(tc, taba, tabb_words, tabb_scales, temper, gw, o
             inv_guess, guess, w0, y = small("inv_guess"), small("guess"), small("w0"), small("y")
             terms = sb.tile([P, TERMS, HALVES, groups], F32, name="terms%d" % u)
             nc.scalar.activation(inv_guess[:], z[:].bitcast(U32), ACT.Exp, bias=biases[:, 0:1], scale=-BITS_SCALE)
-            nc.vector.tensor_scalar(guess[:], z[:].bitcast(I32), -BITS_ONE, BITS_SCALE, ALU.add, ALU.mult)
+            nc.scalar.activation(guess[:], z[:].bitcast(U32), ACT.Identity, bias=biases[:, 2 + len(NODES) : 3 + len(NODES)], scale=BITS_SCALE)
             nc.vector.tensor_tensor(w0[:], z[:], inv_guess[:], ALU.mult)
             for k, t in enumerate(NODES):
                 nc.scalar.activation(terms[:, k], w0[:], ACT.Exp, bias=biases[:, 2 + k : 3 + k], scale=-t / CENTRE)
@@ -140,7 +156,12 @@ def tile_attend_blogpool_kernel(tc, taba, tabb_words, tabb_scales, temper, gw, o
             nc.scalar.activation(th2[:], th[:], ACT.Square)
             nc.vector.scalar_tensor_tensor(gz[:], inv_z[:], -4.0, gw_sb[:, :, j0 // MEMBERS : j1 // MEMBERS], ALU.mult, ALU.mult)
             nc.vector.scalar_tensor_tensor(f[:], th2[:], -1.0, gz[:], ALU.add, ALU.mult)
+            made.append((p, f))
 
+        for u, (j0, j1) in enumerate(UNITS):
+            width = j1 - j0
+            groups = width // MEMBERS
+            p, f = made[u]
             ds = [sb.tile([P, groups, MEMBERS], F32, name="ds%d_%d" % (u, h)) for h in range(HALVES)]
             res = [sb.tile([P, width], F32, name="res%d_%d" % (u, h)) for h in range(HALVES)]
             for h in range(HALVES):

@@ -2,6 +2,7 @@ import math
 from contextlib import ExitStack
 
 import concourse.mybir as mybir
+from concourse.masks import make_identity
 
 D, T, U, I, J, G = 512, 1024, 1024, 256, 512, 64
 FLOPS = 2 * D * I * J
@@ -65,26 +66,33 @@ def tile_attend_blogpool_kernel(tc, taba, tabb_words, tabb_scales, temper, gw, o
     nc = tc.nc
     with ExitStack() as ctx:
         sb = ctx.enter_context(tc.tile_pool(name="sb", bufs=1))
+        late = ctx.enter_context(tc.tile_pool(name="late", bufs=1))
         psum = ctx.enter_context(tc.psum_pool(name="psum", bufs=1))
 
         a_list = sb.tile([P, I // STRIPE], U16, name="a_list")
         b_list = sb.tile([P, J // STRIPE], U16, name="b_list")
         b_scales = sb.tile([P, U], U8, name="b_scales", align_bytes=64)
-        b_words = sb.tile([P, U], U32, name="b_words", align_bytes=64)
-        a_rows = [sb.tile([P, T], F32, name="a_rows%d" % t, align_bytes=64) for t in range(PACK)]
+        seed = late.tile([P, 2 * T + U + HALVES * (J + G)], F32, name="seed", offset=0)
+        a_rows = [sb.tile([P, T], F32, name="a_rows%d" % t, align_bytes=64) for t in range(2)]
+        a_rows.extend(late.tile([P, T], F32, name="a_rows%d" % t, offset=4 * T * (t - 2)) for t in range(2, PACK))
+        b_words = late.tile([P, U], U32, name="b_words", offset=4 * 2 * T)
         temper_sb = sb.tile([P, HALVES], F32, name="temper_sb")
-        gw_sb = sb.tile([P, HALVES, G], F32, name="gw_sb")
-        old_sb = sb.tile([P, HALVES, J], F32, name="old_sb")
+        gw_sb = late.tile([P, HALVES, G], F32, name="gw_sb", offset=4 * (2 * T + U + HALVES * J))
+        old_sb = late.tile([P, HALVES, J], F32, name="old_sb", offset=4 * (2 * T + U))
 
         nc.vector.memset(b_scales[:].bitcast(I32), 0)
+        temper_rows = sb.tile([P, P], F32, name="temper_rows")
+        nc.vector.memset(temper_rows[:], 0.0)
+        nc.vector.memset(seed[:, 0:HALVES], 1.0)
+        minus_one = sb.tile([P, HALVES], F32, name="minus_one")
+        nc.vector.tensor_scalar(minus_one[:], seed[:, 0:HALVES], -1.0, None, ALU.mult)
         ones = sb.tile([P, 1], F32, name="ones")
-        nc.vector.memset(ones[:], 1.0)
+        nc.gpsimd.memset(ones[:], 1.0)
 
         nc.sync.dma_start(b_list[:], offs2)
-        with nc.allow_non_contiguous_dma(reason="one temper a row"):
-            nc.scalar.dma_start(temper_sb[:], temper.rearrange("(h p) o -> p (h o)", h=HALVES))
         for q in range(4):
             nc.scalar.dma_start(b_scales[32 * q : 32 * q + 4, :].bitcast(I32), tabb_scales[0, 4 * q : 4 * q + 4, :].bitcast(I32))
+        nc.scalar.dma_start(temper_rows[0:HALVES, :], temper.rearrange("(h p) o -> h (p o)", h=HALVES))
         nc.sync.dma_start(a_list[:], offs)
         taba_planes = taba.rearrange("(p t) c -> p t c", t=PACK)
         for t in range(PACK):
@@ -96,21 +104,30 @@ def tile_attend_blogpool_kernel(tc, taba, tabb_words, tabb_scales, temper, gw, o
         biases = sb.tile([P, 3 + len(NODES)], F32, name="biases")
         for col, value in enumerate((BITS_ONE * BITS_SCALE, -C0) + tuple(math.log(a) + t for a, t in zip(AMPLITUDES, NODES)) + (-BITS_ONE * BITS_SCALE,)):
             nc.scalar.activation(biases[:, col : col + 1], ones[:], ACT.Copy, scale=value)
+        identity = sb.tile([P, P], F32, name="identity")
+        make_identity(nc, identity[:])
+        turned = psum.tile([P, P], F32, name="turned")
+        nc.tensor.transpose(turned[:], temper_rows[:], identity[:])
+        nc.scalar.copy(temper_sb[:], turned[:, 0:HALVES])
         inv_temper = sb.tile([P, HALVES], F32, name="inv_temper")
-        nc.vector.reciprocal(inv_temper[:], temper_sb[:])
+        nc.gpsimd.tensor_tensor(inv_temper[:], temper_sb[:], minus_one[:], ALU.pow)
         tanh_bias = sb.tile([P, HALVES], F32, name="tanh_bias")
-        nc.vector.tensor_scalar(tanh_bias[:], inv_temper[:], -C0, 2.0, ALU.mult, ALU.add)
+        nc.gpsimd.tensor_scalar(tanh_bias[:], inv_temper[:], -C0, 2.0, ALU.mult, ALU.add)
 
         bg_scales = sb.tile([P, J], U8, name="bg_scales", align_bytes=64)
         nc.vector.tensor_copy(bg_scales[:], b_scales[:].indirect(b_list[:]))
 
         grouped = sb.tile([P, I, PACK], BF16, name="grouped", align_bytes=64)
         dealt = grouped[:].rearrange("p c t -> p t c")
-        for t in range(PACK):
+        for t in range(PACK - 1):
             nc.vector.tensor_copy(dealt[:, t, :], a_rows[t][:].indirect(a_list[:]))
+        for h in range(HALVES):
+            nc.vector.tensor_copy(dealt[:, PACK - 1, h * P : (h + 1) * P], a_rows[PACK - 1][:].indirect(a_list[:, h * P // STRIPE : (h + 1) * P // STRIPE]))
         a_codes = sb.tile([P, I], U32, name="a_codes", align_bytes=64)
         a_scales = sb.tile([P, I], U8, name="a_scales", align_bytes=64)
-        nc.vector.quantize_mx(out=a_codes[:].bitcast(FP8X4), scales=a_scales[:], in_=grouped[:].rearrange("p c t -> p (c t)"))
+        for h in range(HALVES):
+            cols = slice(h * P, (h + 1) * P)
+            nc.vector.quantize_mx(out=a_codes[:, cols].bitcast(FP8X4), scales=a_scales[:, cols], in_=grouped[:, cols, :].rearrange("p c t -> p (c t)"))
 
         out_rows = out.rearrange("(h p) j -> p h j", h=HALVES)
         made = []

import math
from contextlib import ExitStack

import concourse.mybir as mybir
from concourse.masks import make_identity

D, T, U, I, J, G = 512, 1024, 1024, 256, 512, 64
FLOPS = 2 * D * I * J

F32 = mybir.dt.float32
BF16 = mybir.dt.bfloat16
I32 = mybir.dt.int32
U32 = mybir.dt.uint32
U16 = mybir.dt.uint16
U8 = mybir.dt.uint8
FP8X4 = mybir.dt.float8_e4m3fn_x4
ALU = mybir.AluOpType
ACT = mybir.ActivationFunctionType

P = 128
PACK = 4
HALVES = I // P
MEMBERS = J // G
STRIPE = 16
UNITS = ((0, 128), (128, 256), (256, 512))

LN2_SHORT = round(math.log(2.0) * 2.0**16) / 2.0**16
BITS_SCALE = LN2_SHORT / 2.0**23
BITS_ONE = 127.0 * 2.0**23
CENTRE = 1.06
REACH = 0.2
SPACING = 2.0 * REACH / 7.0
SAMPLES = tuple(math.log(1.0 - REACH + n * SPACING) for n in range(8))
CURVES = tuple(2.0 * SAMPLES[n + 1] - SAMPLES[n] - SAMPLES[n + 2] for n in range(6))


def det3(m):
    return sum(m[0][k] * (m[1][(k + 1) % 3] * m[2][(k + 2) % 3] - m[1][(k + 2) % 3] * m[2][(k + 1) % 3]) for k in range(3))


def solve3(m, rhs):
    return tuple(det3([[rhs[r] if c == k else m[r][c] for c in range(3)] for r in range(3)]) / det3(m) for k in range(3))


def bisect_root(poly, low, high):
    for step in range(60):
        middle = (low + high) / 2.0
        low, high = (middle, high) if poly(low) * poly(middle) > 0.0 else (low, middle)
    return low


RECURRENCE = solve3([CURVES[r : r + 3] for r in range(3)], CURVES[3:6])
NODES = tuple(
    bisect_root(lambda t: math.exp(-3.0 * SPACING * t) - sum(c * math.exp(-k * SPACING * t) for k, c in enumerate(RECURRENCE)), low, high)
    for low, high in ((0.1, 2.0), (2.0, 5.0), (5.0, 12.0))
)
CURVE_SHARES = solve3([[math.exp(-r * SPACING * t) for t in NODES] for r in range(3)], CURVES[0:3])
AMPLITUDES = tuple(a * math.exp(-REACH * t) / (1.0 - math.exp(-SPACING * t)) ** 2 for a, t in zip(CURVE_SHARES, NODES))
ENDS = tuple(math.log(1.0 + u) + sum(a * math.exp(-t * u) for a, t in zip(AMPLITUDES, NODES)) for u in (-REACH, REACH))
LINEAR = (ENDS[1] - ENDS[0]) / (2.0 * REACH)
C0 = math.log(CENTRE) - LINEAR + (ENDS[0] + ENDS[1]) / 2.0
TERMS = len(NODES) + 1


def tile_attend_blogpool_kernel(tc, taba, tabb_words, tabb_scales, temper, gw, old, offs, offs2, out):
    nc = tc.nc
    with ExitStack() as ctx:
        sb = ctx.enter_context(tc.tile_pool(name="sb", bufs=1))
        late = ctx.enter_context(tc.tile_pool(name="late", bufs=1))
        psum = ctx.enter_context(tc.psum_pool(name="psum", bufs=1))

        a_list = sb.tile([P, I // STRIPE], U16, name="a_list")
        b_list = sb.tile([P, J // STRIPE], U16, name="b_list")
        b_scales = sb.tile([P, U], U8, name="b_scales", align_bytes=64)
        seed = late.tile([P, 2 * T + U + HALVES * (J + G)], F32, name="seed", offset=0)
        a_rows = [sb.tile([P, T], F32, name="a_rows%d" % t, align_bytes=64) for t in range(2)]
        a_rows.extend(late.tile([P, T], F32, name="a_rows%d" % t, offset=4 * T * (t - 2)) for t in range(2, PACK))
        b_words = late.tile([P, U], U32, name="b_words", offset=4 * 2 * T)
        temper_sb = sb.tile([P, HALVES], F32, name="temper_sb")
        gw_sb = late.tile([P, HALVES, G], F32, name="gw_sb", offset=4 * (2 * T + U + HALVES * J))
        old_sb = late.tile([P, HALVES, J], F32, name="old_sb", offset=4 * (2 * T + U))

        nc.vector.memset(b_scales[:].bitcast(I32), 0)
        temper_rows = sb.tile([P, P], F32, name="temper_rows")
        nc.vector.memset(temper_rows[:], 0.0)
        nc.vector.memset(seed[:, 0:HALVES], 1.0)
        minus_one = sb.tile([P, HALVES], F32, name="minus_one")
        nc.vector.tensor_scalar(minus_one[:], seed[:, 0:HALVES], -1.0, None, ALU.mult)
        ones = sb.tile([P, 1], F32, name="ones")
        nc.gpsimd.memset(ones[:], 1.0)

        nc.sync.dma_start(b_list[:], offs2)
        for q in range(4):
            nc.scalar.dma_start(b_scales[32 * q : 32 * q + 4, :].bitcast(I32), tabb_scales[0, 4 * q : 4 * q + 4, :].bitcast(I32))
        nc.scalar.dma_start(temper_rows[0:HALVES, :], temper.rearrange("(h p) o -> h (p o)", h=HALVES))
        nc.sync.dma_start(a_list[:], offs)
        taba_planes = taba.rearrange("(p t) c -> p t c", t=PACK)
        for t in range(PACK):
            nc.sync.dma_start(a_rows[t][:], taba_planes[:, t, :])
        nc.sync.dma_start(b_words[:].bitcast(I32), tabb_words[0].rearrange("p n t -> p (n t)").bitcast(I32))
        nc.sync.dma_start(gw_sb[:], gw.rearrange("(h p) g -> p h g", h=HALVES))
        nc.sync.dma_start(old_sb[:], old.rearrange("(h p) j -> p h j", h=HALVES))

        biases = sb.tile([P, 3 + len(NODES)], F32, name="biases")
        for col, value in enumerate((BITS_ONE * BITS_SCALE, -C0) + tuple(math.log(a) + t for a, t in zip(AMPLITUDES, NODES)) + (-BITS_ONE * BITS_SCALE,)):
            nc.scalar.activation(biases[:, col : col + 1], ones[:], ACT.Copy, scale=value)
        identity = sb.tile([P, P], F32, name="identity")
        make_identity(nc, identity[:])
        turned = psum.tile([P, P], F32, name="turned")
        nc.tensor.transpose(turned[:], temper_rows[:], identity[:])
        nc.scalar.copy(temper_sb[:], turned[:, 0:HALVES])
        inv_temper = sb.tile([P, HALVES], F32, name="inv_temper")
        nc.gpsimd.tensor_tensor(inv_temper[:], temper_sb[:], minus_one[:], ALU.pow)
        tanh_bias = sb.tile([P, HALVES], F32, name="tanh_bias")
        nc.gpsimd.tensor_scalar(tanh_bias[:], inv_temper[:], -C0, 2.0, ALU.mult, ALU.add)

        bg_scales = sb.tile([P, J], U8, name="bg_scales", align_bytes=64)
        nc.vector.tensor_copy(bg_scales[:], b_scales[:].indirect(b_list[:]))

        grouped = sb.tile([P, I, PACK], BF16, name="grouped", align_bytes=64)
        dealt = grouped[:].rearrange("p c t -> p t c")
        for t in range(PACK - 1):
            nc.vector.tensor_copy(dealt[:, t, :], a_rows[t][:].indirect(a_list[:]))
        for h in range(HALVES):
            nc.vector.tensor_copy(dealt[:, PACK - 1, h * P : (h + 1) * P], a_rows[PACK - 1][:].indirect(a_list[:, h * P // STRIPE : (h + 1) * P // STRIPE]))
        a_codes = sb.tile([P, I], U32, name="a_codes", align_bytes=64)
        a_scales = sb.tile([P, I], U8, name="a_scales", align_bytes=64)
        for h in range(HALVES):
            cols = slice(h * P, (h + 1) * P)
            nc.vector.quantize_mx(out=a_codes[:, cols].bitcast(FP8X4), scales=a_scales[:, cols], in_=grouped[:, cols, :].rearrange("p c t -> p (c t)"))

        out_rows = out.rearrange("(h p) j -> p h j", h=HALVES)
        made = []
        for u, (j0, j1) in enumerate(UNITS):
            width = j1 - j0
            groups = width // MEMBERS

            def small(name):
                return sb.tile([P, HALVES, groups], F32, name="%s%d" % (name, u))

            bg_words = sb.tile([P, width], U32, name="bg_words%d" % u, align_bytes=64)
            nc.vector.tensor_copy(bg_words[:], b_words[:].indirect(b_list[:, j0 // STRIPE : j1 // STRIPE]))
            p = sb.tile([P, HALVES, width], F32, name="p%d" % u)
            z = small("z")
            for h in range(HALVES):
                s = psum.tile([P, width], F32, name="s%d_%d" % (u, h))
                for c0, c1 in ((0, 128), (128, width)) if width == 192 else ((0, width),):
                    nc.tensor.matmul_mx(
                        out=s[:, c0:c1],
                        lhsT=a_codes[:, h * P : (h + 1) * P].bitcast(FP8X4),
                        lhsT_scale=a_scales[:, h * P : (h + 1) * P],
                        rhs=bg_words[:, c0:c1].bitcast(FP8X4),
                        rhs_scale=bg_scales[:, j0 + c0 : j0 + c1],
                        start=True,
                        stop=True,
                    )
                nc.scalar.activation(p[:, h, :], s[:], ACT.Exp, scale=temper_sb[:, h : h + 1])
                nc.vector.tensor_reduce(z[:, h, :], p[:, h, :].rearrange("p (g k) -> p g k", k=MEMBERS), mybir.AxisListType.X, ALU.add)

            inv_guess, guess, w0, y = small("inv_guess"), small("guess"), small("w0"), small("y")
            terms = sb.tile([P, TERMS, HALVES, groups], F32, name="terms%d" % u)
            nc.scalar.activation(inv_guess[:], z[:].bitcast(U32), ACT.Exp, bias=biases[:, 0:1], scale=-BITS_SCALE)
            nc.scalar.activation(guess[:], z[:].bitcast(U32), ACT.Identity, bias=biases[:, 2 + len(NODES) : 3 + len(NODES)], scale=BITS_SCALE)
            nc.vector.tensor_tensor(w0[:], z[:], inv_guess[:], ALU.mult)
            for k, t in enumerate(NODES):
                nc.scalar.activation(terms[:, k], w0[:], ACT.Exp, bias=biases[:, 2 + k : 3 + k], scale=-t / CENTRE)
            nc.vector.scalar_tensor_tensor(terms[:, TERMS - 1], w0[:], -LINEAR / CENTRE, guess[:], ALU.mult, ALU.subtract)
            nc.vector.tensor_reduce(y[:].rearrange("p h g -> p (h g)"), terms[:].rearrange("p k h g -> p (h g) k"), mybir.AxisListType.X, ALU.add)
            th, th2, inv_z, gz, f = small("th"), small("th2"), small("inv_z"), small("gz"), small("f")
            for h in range(HALVES):
                nc.scalar.activation(th[:, h, :], y[:, h, :], ACT.Tanh, bias=tanh_bias[:, h : h + 1], scale=inv_temper[:, h : h + 1])
            nc.scalar.activation(inv_z[:], y[:], ACT.Exp, bias=biases[:, 1:2])
            nc.scalar.activation(th2[:], th[:], ACT.Square)
            nc.vector.scalar_tensor_tensor(gz[:], inv_z[:], -4.0, gw_sb[:, :, j0 // MEMBERS : j1 // MEMBERS], ALU.mult, ALU.mult)
            nc.vector.scalar_tensor_tensor(f[:], th2[:], -1.0, gz[:], ALU.add, ALU.mult)
            made.append((p, f))

        for u, (j0, j1) in enumerate(UNITS):
            width = j1 - j0
            groups = width // MEMBERS
            p, f = made[u]
            ds = [sb.tile([P, groups, MEMBERS], F32, name="ds%d_%d" % (u, h)) for h in range(HALVES)]
            res = [sb.tile([P, width], F32, name="res%d_%d" % (u, h)) for h in range(HALVES)]
            for h in range(HALVES):
                nc.vector.tensor_tensor(
                    ds[h][:],
                    p[:, h, :].rearrange("p (g k) -> p g k", k=MEMBERS),
                    f[:, h, :].unsqueeze(2).to_broadcast([P, groups, MEMBERS]),
                    ALU.mult,
                )
            for h in range(HALVES):
                nc.vector.tensor_tensor(res[h][:], ds[h][:].rearrange("p g k -> p (g k)"), old_sb[:, h, j0:j1], ALU.add)
                nc.sync.dma_start(out_rows[:, h, j0:j1], res[h][:])
